import numpy as np, ml_dtypes
CORES = [83,85,87,115,117,119]
N = 6
import mx_ref
NC, G = 256, 4
C = np.float32(0.043)
WID = [192,128,192,128,256,256]
BF = ml_dtypes.bfloat16
def cut(t, i, w=512):
    return t[:, w * i:w * i + w]
def tile(rs):
    return np.stack(rs, axis=2).reshape(128, -1).astype(BF)
def layer(w, X):
    out = []
    for i in range(G):
        for t in range(len(X)):
            p = mx_ref.matmul(mx_ref.quantize(cut(w, len(X) * i + t)), X[t])
            z = p if t == 0 else z + p
        out.append(z)
    return out
def act(Z):
    return [np.maximum(z, 0) * C for z in Z]
def setup_inputs(rng):
    def f(*shape):
        return mx_ref.flush((rng.standard_normal(shape, dtype=np.float32) * np.exp2(rng.integers(-2, 3, shape[:-1] + (1,)))).astype(BF))
    return {"x": f(N, 128, 4 * NC), "w1": f(N, 128, G * 512), "w2": f(N, 128, 512)}
def setup_inputs_blocks(rng):
    d = setup_inputs(rng)
    for k in ("x", "w1", "w2"): d[k] = mx_ref.spread(d[k], rng, 2)
    return d
def setup_inputs_wide(rng):
    d = setup_inputs(rng)
    for k in ("x", "w1", "w2"): d[k] = mx_ref.flush((d[k].astype(np.float32) * np.exp2(rng.integers(-6, 7, (N, 1, 1))).astype(np.float32)).astype(BF))
    return d
def reference(x, w1, w2):
    X = [mx_ref.quantize(x[j][:, :4 * WID[j]]) for j in range(N)]
    y = np.full((N, 128, NC), np.nan, np.float32)
    for c in range(N):
        for r in range(N):
            p = mx_ref.matmul(mx_ref.quantize(w2[r]), mx_ref.quantize(tile(act(layer(w1[r], [X[c]])))))
            z = p if r == 0 else z + p
        y[c][:, :WID[c]] = z
    return {"y": y}

import numpy as np
from concourse.bass import DstId, RemoteDMATransfer
from concourse.mybir import dt, AluOpType, ActivationFunctionType

SHARE = [
    (0, 0, 192, 3), (2, 128, 64, 3), (1, 0, 128, 4), (2, 0, 128, 5),
    (3, 0, 128, 0), (5, 192, 64, 0), (4, 0, 256, 1), (5, 0, 192, 2),
]
COLS = 384
WT = 640
HALF = 256
C = float(np.float32(0.043))
ZB = 6

SCRATCH = {
    "win": ("sbuf", [128, 2048], "bfloat16"),
    "vin": ("sbuf", [128, 512], "bfloat16"),
    "xin": ("sbuf", [128, 1024], "bfloat16"),
    "xq": ("sbuf", [128, COLS], "float8_e4m3fn_x4"),
    "xs": ("sbuf", [128, COLS], "uint8"),
    "yr": ("sbuf", [128, 256], "float32"),
    "yl": ("sbuf", [128, 256], "float32"),
    "yo": ("sbuf", [128, 256], "float32"),
    "z": ("psum", [128, 512 * ZB], "float32"),
    "acc": ("psum", [128, 1024], "float32"),
}
for _j in range(3):
    SCRATCH["wq%d" % _j] = ("sbuf", [128, WT], "float8_e4m3fn_x4")
    SCRATCH["ws%d" % _j] = ("sbuf", [128, WT], "uint8")
    SCRATCH["h%d" % _j] = ("sbuf", [128, 4 * COLS], "bfloat16")
    SCRATCH["hq%d" % _j] = ("sbuf", [128, COLS], "float8_e4m3fn_x4")
    SCRATCH["hs%d" % _j] = ("sbuf", [128, COLS], "uint8")
SEMAPHORES = ["lA", "lB", "lx", "lv", "qA", "qB", "qx", "qv", "ax", "a0", "a1", "a2", "ay", "sent",
              "accT", "accR", "cR", "yd", "st"]
SEMAPHORES += ["z%d" % k for k in range(24)] + ["e%d" % k for k in range(24)] + ["hq%d" % u for u in range(6)]


def count(mask):
    return bin(mask).count("1")


def rank_program(g, core, T, topo):
    rank = T.rank_of(core)
    if rank is None:
        return
    S = T.sem
    WID = T.tables["WID"]
    cores = T.cores
    local = [r for r in range(len(cores)) if topo.chip(cores[r]) == topo.chip(core)]
    me = local.index(rank)
    nxt, far = (me + 1) % 3, (me + 2) % 3
    own = WID[rank]
    away = [r for r in range(len(cores)) if r not in local]
    on = topo.mask(core, cores[local[nxt]])
    off = topo.mask(core, cores[away[0]])
    rest = on & ~off

    def shares(worker):
        out, at = [], WID[worker]
        for o, a, n, w in SHARE:
            if w == worker:
                out.append((o, a, n, at))
                at += n
        return out

    g.sync.dma_start(T.win[:, 0:4 * HALF], T.w1[:, 0:4 * HALF]).then_inc(S.lA, 16)
    g.scalar.dma_start(T.xin[:, 0:4 * own], T.x[:, 0:4 * own]).then_inc(S.lx, 16)
    g.sync.dma_start(T.win[:, 4 * HALF:2048], T.w1[:, 4 * HALF:2048]).then_inc(S.lB, 16)
    g.scalar.dma_start(T.vin[:], T.w2[:]).then_inc(S.lv, 16)

    wq, ws = T["wq%d" % me], T["ws%d" % me]
    v = g.vector
    v.wait_ge(S.lA, 16)
    v.quantize_mx(wq[:, 0:HALF], ws[:, 0:HALF], T.win[:, 0:4 * HALF]).then_inc(S.qA, 1)
    v.wait_ge(S.lx, 16)
    v.quantize_mx(T.xq[:, 0:own], T.xs[:, 0:own], T.xin[:, 0:4 * own]).then_inc(S.qx, 1)
    v.wait_ge(S.lB, 16)
    v.quantize_mx(wq[:, HALF:512], ws[:, HALF:512], T.win[:, 4 * HALF:2048]).then_inc(S.qB, 1)
    v.wait_ge(S.lv, 16)
    v.quantize_mx(wq[:, 512:WT], ws[:, 512:WT], T.vin[:]).then_inc(S.qv, 1)

    sent = [0]

    def send(dst_ranks, out, src, sem, mask):
        ids = []
        for r in dst_ranks:
            rid, pid, _ = topo.addr(cores[r])
            ids.append(DstId(rid=rid, pnc=pid))
        g.remote_dma_fused([RemoteDMATransfer(dst_ids=ids, dma_engine_mask=mask, remote_sem=sem, srcs=[src],
                                              dsts=[out for _ in ids])], local_sem=S.sent)
        sent[0] += count(mask)

    def codes(t, a, b):
        return t[:, a:b].bitcast(dt.uint8)

    mine = S["a%d" % me]
    g.wait_ge(S.qA, 1)
    send([local[nxt], local[far]], codes(wq, 0, HALF), codes(wq, 0, HALF), mine, rest)
    g.wait_ge(S.qx, 1)
    for w in away:
        for o, a, n, at in shares(w):
            if o == rank:
                send([w], codes(T.xq, at, at + n), codes(T.xq, a, a + n), S.ax, off)
                send([w], T.xs[:, at:at + n], T.xs[:, a:a + n], S.ax, off)
    g.wait_ge(S.qB, 1)
    g.wait_ge(S.qv, 1)
    send([local[nxt]], codes(wq, HALF, WT), codes(wq, HALF, WT), mine, on)
    send([local[nxt], local[far]], ws[:], ws[:], mine, on)
    send([local[far]], codes(wq, HALF, WT), codes(wq, HALF, WT), mine, on)
    W_ARR = count(rest) + 2 * count(on)
    X_ARR = 2 * count(off) * len(shares(rank))
    g.wait_ge(S.cR, 1)
    for o, a, n, at in shares(rank):
        send([o], T.yl[:, a:a + n], T.yr[:, at - own:at - own + n], S.ay, off)
    Y_ARR = count(off) * len([s for s in SHARE if s[0] == rank])

    tok, rem = (0, own), (own, COLS)
    units = [(me, tok), (me, rem), (far, rem), (nxt, rem), (far, tok), (nxt, tok)]
    on_vector = [(1, 3), (1,), (1,), (1, 3), (1,), (1, 3)]

    seen = []

    def need(queue, name, val):
        if (queue, name) not in seen:
            seen.append((queue, name))
            q = g.tensor if queue == "t" else g.vector if queue == "v" else g.scalar
            q.wait_ge(S[name], val)

    def first(u, bs):
        j, (a, b_) = units[u]
        for b in bs:
            k = 4 * u + b
            if j == me:
                need("t", "qA" if b < 2 else "qB", 1)
            else:
                need("t", "a%d" % j, W_ARR)
            if a == 0:
                need("t", "qx", 1)
            else:
                need("t", "ax", X_ARR)
            if k >= ZB:
                need("t", "e%d" % (k - ZB), 1)
            at = 512 * (k % ZB)
            g.tensor.matmul_mx(T.z[:, at:at + b_ - a], T["wq%d" % j][:, 128 * b:128 * b + 128],
                               T["ws%d" % j][:, 128 * b:128 * b + 128], T.xq[:, a:b_], T.xs[:, a:b_],
                               True, True).then_inc(S["z%d" % k], 1)

    def second(u):
        j, (a, b_) = units[u]
        if j == me:
            need("t", "qv", 1)
        need("t", "hq%d" % u, 1)
        at = 0 if a == 0 else 512
        same = [i for i in range(6) if units[i][1] == units[u][1]]
        c = g.tensor.matmul_mx(T.acc[:, at:at + b_ - a], T["wq%d" % j][:, 512:WT], T["ws%d" % j][:, 512:WT],
                               T["hq%d" % j][:, a:b_], T["hs%d" % j][:, a:b_], u == same[0], u == same[-1])
        if u == same[-1]:
            c.then_inc(S.accT if a == 0 else S.accR, 1)

    first(0, (0, 1, 2, 3))
    second(0)
    first(1, (0, 1, 2, 3))
    first(2, (0, 1, 2, 3))
    second(1)
    first(3, (0, 1, 2, 3))
    second(2)
    first(4, (0, 1))
    second(3)
    first(4, (2, 3))
    first(5, (0, 1, 2, 3))
    second(4)
    second(5)

    for u in range(6):
        j, (a, b_) = units[u]
        n = b_ - a
        h = T["h%d" % j]
        for b in range(4):
            k = 4 * u + b
            at = 512 * (k % ZB)
            src, dst = T.z[:, at:at + n], h[:, 4 * a + b:4 * b_:4]
            if b in on_vector[u]:
                need("v", "z%d" % k, 1)
                v.tensor_scalar(dst, src, 0.0, C, AluOpType.max, AluOpType.mult).then_inc(S["e%d" % k], 1)
            else:
                need("s", "z%d" % k, 1)
                g.scalar.activation(dst, src, ActivationFunctionType.Relu, scale=C).then_inc(S["e%d" % k], 1)
        for b in range(4):
            need("v", "e%d" % (4 * u + b), 1)
        v.quantize_mx(T["hq%d" % j][:, a:b_], T["hs%d" % j][:, a:b_], h[:, 4 * a:4 * b_]).then_inc(S["hq%d" % u], 1)
        if u == 3:
            need("v", "accR", 1)
            v.tensor_copy(T.yr[:, 0:COLS - own], T.acc[:, 512:512 + COLS - own]).then_inc(S.cR, 1)

    need("v", "accT", 1)
    need("v", "ay", Y_ARR)
    v.tensor_tensor(T.yo[:, 0:own], T.acc[:, 0:own], T.yl[:, 0:own], AluOpType.add).then_inc(S.yd, 1)
    g.sync.wait_ge(S.yd, 1)
    g.sync.dma_start(T.y[:, 0:own], T.yo[:, 0:own]).then_inc(S.st, 16)
    g.sync.wait_ge(S.st, 16)
    g.wait_ge(S.sent, sent[0])
